import numpy as np
import ml_dtypes


def mxq(x, axis, fmt="e4m3"):
    dtype, down = {"e4m3": (ml_dtypes.float8_e4m3fn, 7), "e5m2": (ml_dtypes.float8_e5m2, 14)}[fmt]
    v = np.moveaxis(np.asarray(x, np.float32).astype(ml_dtypes.bfloat16).astype(np.float64), axis, -1)
    blocks = v.reshape(v.shape[:-1] + (-1, 32))
    amax = np.abs(blocks).max(-1, keepdims=True)
    byte = np.maximum(np.where(amax > 0, np.frexp(amax)[1] - 1 + 127, 0) - down, 1)
    scale = np.exp2(byte - 127.0)
    codes = (blocks / scale).astype(np.float32).astype(dtype).astype(np.float64)
    return np.moveaxis((codes * scale).reshape(v.shape), -1, axis)


WIDE = False


def mx_kscale(k):
    if not WIDE:
        return np.ones(k)
    levels = np.array([10, -10, 5, -5, 0])
    if k % 512:
        return np.exp2(np.random.permutation(np.resize(levels, k // 32))).repeat(32)
    a = np.empty((k // 512, 16))
    for p in range(k // 512):
        a[p, :8] = np.random.permutation(np.resize(levels, 8))
        for g in range(8):
            far = levels[np.abs(levels - a[p, g]) >= 10]
            a[p, g + 8] = far[np.random.randint(len(far))]
    return np.exp2(a.ravel()).repeat(32)


BF16 = ml_dtypes.bfloat16


def bf(x):
    return np.asarray(x, np.float32).astype(BF16)


def f64(x):
    return np.asarray(x).astype(np.float64)


E2M1 = np.array([0.0, 0.5, 1.0, 1.5, 2.0, 3.0, 4.0, 6.0, -0.0, -0.5, -1.0, -1.5, -2.0, -3.0, -4.0, -6.0])


def pack_weight(w, fmt):
    k, n = w.shape
    w = f64(bf(w)).reshape(k // 32, 32, n)
    amax = np.abs(w).max(1)
    if fmt == "e4m3":
        byte = np.frexp(amax)[1] - 1 + 127 - 7
    else:
        mant, ex = np.frexp(amax / 6.0)
        byte = np.where(mant > 0.5, ex, ex - 1) + 127
    byte = np.clip(np.where(amax > 0, byte, 1), 1, 254)
    scaled = (w * np.exp2(127.0 - byte)[:, None, :]).reshape(k, n).astype(np.float32)
    by_word = np.ascontiguousarray(scaled.reshape(k // 512, 128, 4, n).transpose(0, 1, 3, 2))
    if fmt == "e4m3":
        words = by_word.astype(ml_dtypes.float8_e4m3fn).view(np.uint8)
    else:
        c = by_word.astype(ml_dtypes.float4_e2m1fn).view(np.uint8) & 0xF
        words = c[..., 0::2] | (c[..., 1::2] << 4)
    return np.ascontiguousarray(words), np.ascontiguousarray(byte.astype(np.uint8).reshape(k // 512, 16, n))


def unpack_weight(words, scales, fmt):
    g, p, n, _ = words.shape
    if fmt == "e4m3":
        vals = np.ascontiguousarray(words).view(ml_dtypes.float8_e4m3fn).astype(np.float64)
    else:
        nib = np.empty((g, p, n, 4), np.uint8)
        nib[..., 0::2] = words & 0xF
        nib[..., 1::2] = words >> 4
        vals = E2M1[nib]
    vals = vals * np.repeat(np.exp2(scales.astype(np.float64) - 127.0), 8, axis=1)[..., None]
    return vals.transpose(0, 1, 3, 2).reshape(g * 512, n)

E4M3FN = np.array([(-1.0 if i & 128 else 1.0) * ((1.0 + (i & 7) / 8.0) * 2.0 ** (((i >> 3) & 15) - 7) if i & 120 else (i & 7) * 2.0 ** -9) for i in range(256)])


def e4m3fn_bytes(y):
    return np.clip(np.asarray(y, np.float64), -448.0, 448.0).astype(np.float32).astype(ml_dtypes.float8_e4m3fn).view(np.uint8)


def e4m3fn_values(b):
    return E4M3FN[b]


B, L, D, F, DO = 2, 1024, 1024, 1024, 1024
BLOCKS = (1, 2, 4, 8)


def block_mean_repeat(h, b):
    if b == 1:
        return h
    n, length, f = h.shape
    means = np.mean(h.reshape(n, length // b, b, f), axis=2)
    return np.repeat(means, b, axis=1)


def softmax_last(v):
    e = np.exp(v - v.max(axis=-1, keepdims=True))
    return e / e.sum(axis=-1, keepdims=True)


def draw0():
    s, t = mx_kscale(D), mx_kscale(F)
    x = bf(np.random.standard_normal((B, L, D)) * s)
    w1_words, w1_scales = pack_weight(np.random.standard_normal((D, F)) / np.sqrt(D) / s[:, None] * t, "e4m3")
    b1 = bf(np.random.standard_normal(F) * 0.3 * t)
    ws = bf(2.0 * np.random.standard_normal(F) / np.sqrt(F) / t)
    w2_words, w2_scales = pack_weight(1.5 * np.random.standard_normal((F, DO)) / np.sqrt(F) / t[:, None], "e4m3")
    return {"x": x,
            "w1_words": w1_words,
            "w1_scales": w1_scales,
            "b1": b1,
            "ws": ws,
            "w2_words": w2_words,
            "w2_scales": w2_scales}


def core(x, w1_words, w1_scales, b1, ws, w2_words, w2_scales):
    h = (mxq(f64(x), 2, "e4m3") @ unpack_weight(w1_words, w1_scales, "e4m3")) + f64(b1)
    wsf = f64(ws)

    cands = []
    scores = []
    for b in BLOCKS:
        p = block_mean_repeat(h, b)
        cands.append(p)
        scores.append(np.sum(p * wsf, axis=-1))
    sc = np.stack(scores, axis=-1)

    a = softmax_last(sc)

    m = np.zeros_like(h)
    for i, p in enumerate(cands):
        m = m + a[:, :, i, None] * p

    d = 0.5 * (m[:, 0::2, :] + m[:, 1::2, :])

    return mxq(d, 2, "e4m3") @ unpack_weight(w2_words, w2_scales, "e4m3")


def setup_inputs():
    drawn = draw0()
    full = np.asarray(drawn['x']).astype(np.float64)
    scale = (np.abs(full).reshape(2, 1024, 8, 128).max(axis=(3,)) / 448.0).astype(np.float32)
    given = {}
    for key, value in drawn.items():
        if key == 'x':
            given['x_bytes'] = e4m3fn_bytes(full / np.repeat(scale.astype(np.float64), 128, axis=2))
            given['x_scale'] = scale
        else:
            given[key] = value
    return given


def reference(x_bytes, x_scale, w1_words, w1_scales, b1, ws, w2_words, w2_scales):
    return core(e4m3fn_values(x_bytes) * np.repeat(x_scale.astype(np.float64), 128, axis=2), w1_words, w1_scales, b1, ws, w2_words, w2_scales)

@@ -1,0 +1,332 @@
+from contextlib import ExitStack
+
+import concourse.mybir as mybir
+from concourse.masks import make_identity
+
+F32 = mybir.dt.float32
+BF16 = mybir.dt.bfloat16
+U32 = mybir.dt.uint32
+I32 = mybir.dt.int32
+U8 = mybir.dt.uint8
+F8 = mybir.dt.float8_e4m3fn
+F8X4 = mybir.dt.float8_e4m3fn_x4
+ALU = mybir.AluOpType
+ACT = mybir.ActivationFunctionType
+AX = mybir.AxisListType
+
+P = 128
+TOKENS, D, F, DO = 2048, 1024, 1024, 1024
+NU = 8
+TPU = 2
+FLOPS = 2 * TOKENS * D * F + 2 * (TOKENS // 2) * F * DO
+VW = (3, 5, 8, 8, 5, 0, 3, 1)
+STEP = (
+    ("quant_x", 1, (0,)),
+    ("ocopy", -3, (1,)),
+    ("mix", -2, (0,)),
+    ("score", -1, (1,)),
+    ("xcopy", 2, (0,)),
+    ("quant_x", 0, (1,)),
+    ("widen", 3, (0,)),
+    ("mix", -2, (1,)),
+    ("spread", -1, ()),
+    ("score", 0, (0,)),
+    ("stage1", 0, (1,)),
+    ("add_bias", -2, (0,)),
+    ("add_bias", -2, (1,)),
+    ("gather", -1, ()),
+    ("soft_a", -1, ()),
+    ("stage1", 1, (0,)),
+    ("turn", 2, (1,)),
+    ("widen", 3, (1,)),
+    ("turn", 3, (0,)),
+    ("quant_d", -2, ()),
+    ("stage2", -2, (0,)),
+    ("stage2", -2, (1,)),
+    ("ocopy", -2, (0,)),
+    ("xcopy", 2, (1,)),
+    ("soft_b", -1, ()),
+)
+
+
+def tile_charformersoftsubwordblockmixer_d1p_kernel(
+    tc, x_bytes, x_scale, w1_words, w1_scales, b1, ws, w2_words, w2_scales, out
+):
+    nc = tc.nc
+    with ExitStack() as ctx:
+        keep = ctx.enter_context(tc.tile_pool(name="keep", bufs=1))
+        xin = ctx.enter_context(tc.tile_pool(name="xin", bufs=8))
+        work = ctx.enter_context(tc.tile_pool(name="work", bufs=3))
+        small = ctx.enter_context(tc.tile_pool(name="small", bufs=3))
+        psum = ctx.enter_context(tc.psum_pool(name="psum", bufs=1))
+
+        x_rows = x_bytes.flatten_outer_dims().rearrange("(u i p) d -> u p i d", i=TPU, p=P)
+        out_rows = out.flatten_outer_dims().rearrange("(u p) d -> u p d", p=P)
+
+        ident = keep.tile([P, P], F32, name="ident", align_bytes=64)
+        xs = keep.tile([P, NU * TPU, 8], F32, name="xs")
+        w1c = keep.tile([P, 2, F], U32, name="w1c", align_bytes=64)
+        w2c = keep.tile([P, 2, DO], U32, name="w2c", align_bytes=64)
+        w1s = keep.tile([P, F], U8, name="w1s", align_bytes=64)
+        w2s = keep.tile([P, DO], U8, name="w2s", align_bytes=64)
+        wrow = keep.tile([P, F], BF16, name="wrow", align_bytes=64)
+        ones = keep.tile([P, P], BF16, name="ones", align_bytes=64)
+        wsb = keep.tile([P, F], F32, name="wsb", align_bytes=64)
+        b1pt = keep.tile([P, 2, 4], BF16, name="b1pt")
+        r1 = keep.tile([P, 8], F32, name="r1")
+        p2 = keep.tile([P, 4], F32, name="p2")
+        p4 = keep.tile([P, 2], F32, name="p4")
+        rm = keep.tile([P, 8, 4], F32, name="rm")
+        g16 = keep.tile([P, 16], F32, name="g16")
+        gm = keep.tile([P, 16], F32, name="gm")
+        bones = keep.tile([P, 16, 8], F32, name="bones", align_bytes=64)
+        warm = keep.tile([P, 1], F32, name="warm")
+
+        xb, xw, xt, xg, xc, xsc, hp, hsb, sv, rs, sc, ek, ct, mp, dg, dc, dsc, om, osb = ({} for _ in range(19))
+
+        def load_x(u):
+            xb[u] = xin.tile([P, TPU, D], U8, name="xb", align_bytes=64)
+            nc.sync.dma_start(out=xb[u][:], in_=x_rows[u])
+
+        def widen(u, part):
+            if part == 0:
+                xw[u] = work.tile([P, TPU, D], BF16, name="xw", align_bytes=64)
+            for b in range(8):
+                i, j = part, b
+                cols = slice(128 * j, 128 * j + 128)
+                src = xb[u][:, i, cols].bitcast(F8)
+                sc = xs[:, TPU * u + i, j : j + 1]
+                if b < VW[u]:
+                    nc.vector.tensor_scalar(out=xw[u][:, i, cols], in0=src, scalar1=sc, scalar2=None, op0=ALU.mult)
+                else:
+                    nc.scalar.activation(out=xw[u][:, i, cols], in_=src, func=ACT.Copy, scale=sc)
+
+        def turn(u, i):
+            xt[u, i] = psum.tile([P, 2, 2, P], F32, name="xt", bufs=2)
+            words = xw[u][:, i, :].bitcast(F32)
+            for g in range(2):
+                for e in range(2):
+                    nc.tensor.transpose(xt[u, i][:, g, e, :], words[:, 256 * g + e : 256 * (g + 1) : 2], ident[:])
+
+        def xcopy(u, i):
+            if i == 0:
+                xg[u] = work.tile([P, TPU, 2, P, 2], F32, name="xg", align_bytes=64)
+            nc.scalar.copy(out=xg[u][:, i], in_=xt[u, i][:].rearrange("p g e r -> p g r e"))
+
+        def quant_x(u, i):
+            if i == 0:
+                xc[u] = work.tile([P, TPU, 2, P], U32, name="xc", align_bytes=64)
+                xsc[u] = work.tile([P, TPU, 2, P], U8, name="xsc", align_bytes=64)
+            nc.vector.quantize_mx(
+                out=xc[u][:, i].rearrange("p g r -> p (g r)").bitcast(F8X4),
+                scales=xsc[u][:, i].rearrange("p g r -> p (g r)"),
+                in_=xg[u][:, i].rearrange("p g r e -> p (g r e)").bitcast(BF16),
+            )
+
+        def stage1(u, i):
+            for n in range(2):
+                hp[u, i, n] = psum.tile([P, 512], F32, name="mm", bufs=3)
+                cols = slice(512 * n, 512 * n + 512)
+                for g in range(2):
+                    nc.tensor.matmul_mx(
+                        out=hp[u, i, n][:],
+                        lhsT=xc[u][:, i, g, :].bitcast(F8X4),
+                        lhsT_scale=xsc[u][:, i, g, :],
+                        rhs=w1c[:, g, cols].bitcast(F8X4),
+                        rhs_scale=w1s[4 * g : P, cols],
+                        start=(g == 0),
+                        stop=(g == 1),
+                    )
+                if n == 0:
+                    hcopy(u, i, 0)
+            hcopy(u, i, 1)
+
+        def hcopy(u, i, n):
+            if i == 0 and n == 0:
+                hsb[u] = work.tile([P, TPU, F], F32, name="hsb", bufs=4, align_bytes=64)
+            nc.scalar.copy(
+                out=hsb[u][:, i, 512 * n : 512 * n + 512].rearrange("q (t p) -> q t p", t=4),
+                in_=hp[u, i, n][:].rearrange("q (p t) -> q t p", t=4),
+            )
+
+        def score(u, i):
+            if i == 0:
+                sv[u] = small.tile([P, TPU], F32, name="sv")
+            junk = work.tile([P, F], F32, name="junk", bufs=2)
+            nc.vector.scalar_tensor_tensor(
+                out=junk[:], in0=hsb[u][:, i, :], scalar=1.0, in1=wsb[:],
+                op0=ALU.mult, op1=ALU.mult, accum_out=sv[u][:, i : i + 1],
+            )
+
+        def spread(u):
+            rs[u] = small.tile([P, TPU, 32], F32, name="rs", align_bytes=64)
+            nc.vector.tensor_tensor(
+                out=rs[u][:],
+                in0=rm[:].rearrange("p r b -> p (r b)").unsqueeze(1).to_broadcast([P, TPU, 32]),
+                in1=sv[u][:].unsqueeze(2).to_broadcast([P, TPU, 32]),
+                op=ALU.mult,
+            )
+
+        def gather(u):
+            sc[u] = psum.tile([P, 64], F32, name="sc", bufs=1)
+            nc.tensor.matmul(
+                sc[u][:], lhsT=bones[:].rearrange("p g r -> p (g r)"),
+                rhs=rs[u][:].rearrange("p i c -> p (i c)"), start=True, stop=True,
+            )
+
+        def soft_a(u):
+            s3 = sc[u][:].rearrange("p (m b) -> p m b", b=4)
+            mx = small.tile([P, 16], F32, name="mx")
+            nc.vector.tensor_reduce(out=mx[:], in_=s3, axis=AX.X, op=ALU.max)
+            df = small.tile([P, 16, 4], F32, name="df")
+            nc.vector.tensor_tensor(out=df[:], in0=s3, in1=mx[:].unsqueeze(2).to_broadcast([P, 16, 4]), op=ALU.subtract)
+            ek[u] = small.tile([P, 2, 64], F32, name="ek")
+            nc.scalar.activation(out=ek[u][:, 0, :], in_=df[:].rearrange("p m b -> p (m b)"), func=ACT.Exp)
+
+        def soft_b(u):
+            nc.vector.tensor_tensor(
+                out=ek[u][:, 1, :].rearrange("p (i c) -> p i c", i=TPU),
+                in0=ek[u][:, 0, :].rearrange("p (i c) -> p i c", i=TPU),
+                in1=rm[:].rearrange("p r b -> p (r b)").unsqueeze(1).to_broadcast([P, TPU, 32]),
+                op=ALU.mult,
+            )
+            dn = small.tile([P, 32], F32, name="dn")
+            nc.vector.tensor_reduce(out=dn[:], in_=ek[u][:].rearrange("p c (m b) -> p (c m) b", b=4), axis=AX.X, op=ALU.add)
+            rd = small.tile([P, 16], F32, name="rd")
+            nc.vector.reciprocal(out=rd[:], in_=dn[:, 0:16])
+            wt = small.tile([P, 16], F32, name="wt")
+            nc.vector.tensor_tensor(out=wt[:], in0=dn[:, 16:32], in1=rd[:], op=ALU.mult)
+            cc = small.tile([P, TPU, 4], F32, name="cc")
+            nc.vector.tensor_reduce(
+                out=cc[:].rearrange("p i j -> p (i j)"), in_=wt[:].rearrange("p (m r) -> p m r", r=2), axis=AX.X, op=ALU.add
+            )
+            ct[u] = small.tile([P, TPU, 16, 4], F32, name="ct", align_bytes=64)
+            nc.vector.tensor_tensor(
+                out=ct[u][:],
+                in0=gm[:].unsqueeze(1).unsqueeze(3).to_broadcast([P, TPU, 16, 4]),
+                in1=cc[:].unsqueeze(2).to_broadcast([P, TPU, 16, 4]),
+                op=ALU.mult,
+            )
+
+        def mix(u, g):
+            mp[u, g] = psum.tile([P, 4, TPU, 64], F32, name="mp", bufs=2)
+            for i in range(TPU):
+                for t in range(4):
+                    c0 = 512 * g + 128 * t
+                    nc.tensor.matmul(
+                        mp[u, g][:, t, i, :], lhsT=hsb[u][:, i, c0 : c0 + 128],
+                        rhs=ct[u][:, i].rearrange("p a b -> p (a b)"), start=True, stop=True,
+                    )
+
+        def add_bias(u, g):
+            if g == 0:
+                dg[u] = work.tile([P, 2, P, 4], BF16, name="dg", align_bytes=64)
+            nc.vector.tensor_tensor(
+                out=dg[u][:, g],
+                in0=mp[u, g][:].rearrange("p t i n -> p (i n) t"),
+                in1=b1pt[:, g, :].unsqueeze(1).to_broadcast([P, P, 4]),
+                op=ALU.add,
+            )
+
+        def quant_d(u):
+            dc[u] = work.tile([P, 2, P], U32, name="dc", align_bytes=64)
+            dsc[u] = work.tile([P, 2, P], U8, name="dsc", align_bytes=64)
+            nc.vector.quantize_mx(
+                out=dc[u][:].rearrange("p g r -> p (g r)").bitcast(F8X4),
+                scales=dsc[u][:].rearrange("p g r -> p (g r)"),
+                in_=dg[u][:].rearrange("p g r e -> p (g r e)"),
+            )
+
+        def stage2(u, n):
+            om[u, n] = psum.tile([P, 512], F32, name="mm", bufs=3)
+            cols = slice(512 * n, 512 * n + 512)
+            for g in range(2):
+                nc.tensor.matmul_mx(
+                    out=om[u, n][:],
+                    lhsT=dc[u][:, g, :].bitcast(F8X4),
+                    lhsT_scale=dsc[u][:, g, :],
+                    rhs=w2c[:, g, cols].bitcast(F8X4),
+                    rhs_scale=w2s[4 * g : P, cols],
+                    start=(g == 0),
+                    stop=(g == 1),
+                )
+
+        def ocopy(u, n):
+            if n == 0:
+                osb[u] = work.tile([P, DO], F32, name="osb", align_bytes=64)
+            nc.scalar.copy(out=osb[u][:, 512 * n : 512 * n + 512], in_=om[u, n][:])
+            if n == 1:
+                nc.sync.dma_start(out=out_rows[u], in_=osb[u][:])
+
+        def load_scales(tile, dram):
+            for q in range(4):
+                nc.sync.dma_start(
+                    out=tile[32 * q : 32 * q + 8, :].bitcast(I32),
+                    in_=dram[:, 4 * q : 4 * q + 4, :].bitcast(I32),
+                )
+
+        def load_words(tile, dram):
+            for g in range(2):
+                nc.sync.dma_start(
+                    out=tile[:, g, :].bitcast(I32), in_=dram[g].rearrange("p n t -> p (n t)").bitcast(I32)
+                )
+
+        ops = {
+            "widen": widen, "turn": turn, "xcopy": xcopy, "quant_x": quant_x, "stage1": stage1, "score": score,
+            "spread": spread, "gather": gather, "soft_a": soft_a, "soft_b": soft_b, "mix": mix, "add_bias": add_bias,
+            "quant_d": quant_d, "stage2": stage2, "ocopy": ocopy,
+        }
+
+        with tc.manual_schedule():
+            nc.scalar.dma_start(out=xs[:], in_=x_scale.flatten_outer_dims().rearrange("(n p) s -> p n s", p=P))
+            load_x(0)
+            make_identity(nc, ident[:])
+            nc.vector.memset(w1s[:].bitcast(I32), 0)
+            nc.vector.memset(w2s[:].bitcast(I32), 0)
+            nc.vector.memset(wrow[:].bitcast(I32), 0)
+            nc.vector.memset(ones[:], 1.0)
+            nc.vector.memset(warm[:], 0.0)
+            nc.scalar.dma_start(out=wrow[0:1, :], in_=ws.rearrange("(o f) -> o f", o=1))
+            nc.scalar.dma_start(out=b1pt[:], in_=b1.rearrange("(g p t) -> p g t", p=P, t=4))
+            nc.scalar.activation(out=warm[:], in_=warm[:], func=ACT.Exp)
+            load_scales(w1s, w1_scales)
+            load_scales(w2s, w2_scales)
+            load_words(w1c, w1_words)
+            load_x(1)
+            load_x(2)
+            load_x(3)
+            load_words(w2c, w2_words)
+            for u in range(4, NU):
+                load_x(u)
+
+            nc.vector.tensor_reduce(out=r1[:], in_=ident[:].rearrange("p (g r) -> p r g", r=8), axis=AX.X, op=ALU.add)
+            nc.vector.tensor_reduce(out=g16[:], in_=ident[:].rearrange("p (g r) -> p g r", r=8), axis=AX.X, op=ALU.add)
+            nc.vector.tensor_reduce(out=p2[:], in_=r1[:].rearrange("p (q c) -> p q c", c=2), axis=AX.X, op=ALU.add)
+            nc.vector.tensor_reduce(out=p4[:], in_=p2[:].rearrange("p (q c) -> p q c", c=2), axis=AX.X, op=ALU.add)
+            nc.vector.tensor_copy(out=rm[:, :, 0], in_=r1[:])
+            nc.vector.tensor_scalar(
+                out=rm[:, :, 1].rearrange("p (q c) -> p q c", c=2), in0=p2[:].unsqueeze(2).to_broadcast([P, 4, 2]),
+                scalar1=0.5, scalar2=None, op0=ALU.mult,
+            )
+            nc.vector.tensor_scalar(
+                out=rm[:, :, 2].rearrange("p (q c) -> p q c", c=4), in0=p4[:].unsqueeze(2).to_broadcast([P, 2, 4]),
+                scalar1=0.25, scalar2=None, op0=ALU.mult,
+            )
+            nc.vector.memset(rm[:, :, 3], 0.125)
+            nc.vector.tensor_scalar(out=gm[:], in0=g16[:], scalar1=0.5, scalar2=None, op0=ALU.mult)
+            nc.vector.tensor_copy(out=bones[:], in_=g16[:].unsqueeze(2).to_broadcast([P, 16, 8]))
+
+            for n in range(2):
+                cols = slice(512 * n, 512 * n + 512)
+                wp = psum.tile([P, 512], F32, name="mm", bufs=3)
+                nc.tensor.matmul(wp[:], lhsT=ones[:], rhs=wrow[:, cols], start=True, stop=True)
+                nc.scalar.copy(
+                    out=wsb[:, cols].rearrange("q (t p) -> q t p", t=4), in_=wp[:].rearrange("q (p t) -> q t p", t=4)
+                )
+
+            first = -max(lag for name, lag, args in STEP)
+            last = NU - min(lag for name, lag, args in STEP)
+            for k in range(first, last):
+                for name, lag, args in STEP:
+                    if 0 <= k + lag < NU:
+                        ops[name](k + lag, *args)

@@ -19,33 +19,54 @@ TOKENS, D, F, DO = 2048, 1024, 1024, 1024
 NU = 8
 TPU = 2
 FLOPS = 2 * TOKENS * D * F + 2 * (TOKENS // 2) * F * DO
-VW = (3, 5, 8, 8, 5, 0, 3, 1)
+WS_STEP = 0
+MMB, XTB, MPB = 3, 2, 2
+VW = (5, 5, 7, 8, 3, 6, 4, 5)
 STEP = (
-    ("quant_x", 1, (0,)),
-    ("ocopy", -3, (1,)),
-    ("mix", -2, (0,)),
+    ("soft", -2, (3,)),
+    ("turn", 0, (0,)),
+    ("score", -1, (0,)),
+    ("mix", -3, (1,)),
+    ("turn", 0, (1,)),
+    ("soft", -2, (4,)),
+    ("xcopy", 0, (0,)),
     ("score", -1, (1,)),
-    ("xcopy", 2, (0,)),
+    ("quant_x", 0, (0,)),
+    ("soft", -2, (5,)),
+    ("stage2", -5, (0,)),
+    ("spread", -1, (0,)),
+    ("xcopy", 0, (1,)),
+    ("soft", -2, (6,)),
+    ("spread", -1, (1,)),
+    ("pair_mean", -3, (0,)),
+    ("ocopy", -5, (0,)),
+    ("soft", -2, (7,)),
+    ("stage2", -5, (1,)),
     ("quant_x", 0, (1,)),
-    ("widen", 3, (0,)),
-    ("mix", -2, (1,)),
-    ("spread", -1, ()),
-    ("score", 0, (0,)),
-    ("stage1", 0, (1,)),
-    ("add_bias", -2, (0,)),
-    ("add_bias", -2, (1,)),
+    ("soft", -2, (8,)),
+    ("pair_mean", -3, (1,)),
+    ("stage1", 0, (0, 0)),
+    ("ocopy", -5, (1,)),
+    ("widen", 1, (0, True)),
+    ("hcopy", 0, (0, 0)),
     ("gather", -1, ()),
-    ("soft_a", -1, ()),
-    ("stage1", 1, (0,)),
-    ("turn", 2, (1,)),
-    ("widen", 3, (1,)),
-    ("turn", 3, (0,)),
-    ("quant_d", -2, ()),
-    ("stage2", -2, (0,)),
-    ("stage2", -2, (1,)),
-    ("ocopy", -2, (0,)),
-    ("xcopy", 2, (1,)),
-    ("soft_b", -1, ()),
+    ("stage1", 0, (0, 1)),
+    ("stage1", 0, (1, 0)),
+    ("widen", 1, (1, True)),
+    ("soft", -1, (0,)),
+    ("hcopy", 0, (0, 1)),
+    ("quant_d", -4, ()),
+    ("soft", -1, (1,)),
+    ("soft", -1, (2,)),
+    ("widen", 2, (0, False)),
+    ("stage1", 0, (1, 1)),
+    ("soft", -2, (9,)),
+    ("mix", -2, (0,)),
+    ("turn_d", -3, ()),
+    ("hcopy", 0, (1, 0)),
+    ("hcopy", 0, (1, 1)),
+    ("widen", 2, (1, False)),
+    ("dcopy", -3, ()),
 )
 
 
@@ -57,14 +78,14 @@ def tile_charformersoftsubwordblockmixer_d1p_kernel(
         keep = ctx.enter_context(tc.tile_pool(name="keep", bufs=1))
         xin = ctx.enter_context(tc.tile_pool(name="xin", bufs=8))
         work = ctx.enter_context(tc.tile_pool(name="work", bufs=3))
-        small = ctx.enter_context(tc.tile_pool(name="small", bufs=3))
+        small = ctx.enter_context(tc.tile_pool(name="small", bufs=6))
         psum = ctx.enter_context(tc.psum_pool(name="psum", bufs=1))
 
-        x_rows = x_bytes.flatten_outer_dims().rearrange("(u i p) d -> u p i d", i=TPU, p=P)
+        x_rows = x_bytes.flatten_outer_dims().rearrange("(u p i) d -> u p i d", i=TPU, p=P)
         out_rows = out.flatten_outer_dims().rearrange("(u p) d -> u p d", p=P)
 
         ident = keep.tile([P, P], F32, name="ident", align_bytes=64)
-        xs = keep.tile([P, NU * TPU, 8], F32, name="xs")
+        xs = keep.tile([P, NU, TPU, 8], F32, name="xs")
         w1c = keep.tile([P, 2, F], U32, name="w1c", align_bytes=64)
         w2c = keep.tile([P, 2, DO], U32, name="w2c", align_bytes=64)
         w1s = keep.tile([P, F], U8, name="w1s", align_bytes=64)
@@ -72,37 +93,37 @@ def tile_charformersoftsubwordblockmixer_d1p_kernel(
         wrow = keep.tile([P, F], BF16, name="wrow", align_bytes=64)
         ones = keep.tile([P, P], BF16, name="ones", align_bytes=64)
         wsb = keep.tile([P, F], F32, name="wsb", align_bytes=64)
-        b1pt = keep.tile([P, 2, 4], BF16, name="b1pt")
-        r1 = keep.tile([P, 8], F32, name="r1")
-        p2 = keep.tile([P, 4], F32, name="p2")
-        p4 = keep.tile([P, 2], F32, name="p4")
-        rm = keep.tile([P, 8, 4], F32, name="rm")
-        g16 = keep.tile([P, 16], F32, name="g16")
-        gm = keep.tile([P, 16], F32, name="gm")
-        bones = keep.tile([P, 16, 8], F32, name="bones", align_bytes=64)
+        brow = keep.tile([P, F], BF16, name="brow", align_bytes=64)
+        q4 = keep.tile([P, 4], F32, name="q4")
+        h2 = keep.tile([P, 2], F32, name="h2")
+        mo = keep.tile([P, 8, 4], F32, name="mo")
+        md = keep.tile([P, 8, 4], F32, name="md")
+        g32 = keep.tile([P, 32], F32, name="g32")
+        gm = keep.tile([P, 32], F32, name="gm")
+        bones = keep.tile([P, 32, 4], F32, name="bones", align_bytes=64)
         warm = keep.tile([P, 1], F32, name="warm")
 
-        xb, xw, xt, xg, xc, xsc, hp, hsb, sv, rs, sc, ek, ct, mp, dg, dc, dsc, om, osb = ({} for _ in range(19))
+        xb, xw, xt, xg, xc, xsc, hp, he, hs, s_t, r0, rs, sc = ({} for _ in range(13))
+        mx, df, ex, dn, rd, aw, ak, cc, ct, de, mp, db, dt, dg, dc, dsc, om, osb = ({} for _ in range(18))
 
         def load_x(u):
             xb[u] = xin.tile([P, TPU, D], U8, name="xb", align_bytes=64)
             nc.sync.dma_start(out=xb[u][:], in_=x_rows[u])
 
-        def widen(u, part):
-            if part == 0:
-                xw[u] = work.tile([P, TPU, D], BF16, name="xw", align_bytes=64)
-            for b in range(8):
-                i, j = part, b
+        def widen(u, i, vector):
+            if u not in xw:
+                xw[u] = work.tile([P, TPU, D], BF16, name="xw", bufs=4, align_bytes=64)
+            for j in range(0, VW[u]) if vector else range(VW[u], 8):
                 cols = slice(128 * j, 128 * j + 128)
                 src = xb[u][:, i, cols].bitcast(F8)
-                sc = xs[:, TPU * u + i, j : j + 1]
-                if b < VW[u]:
+                sc = xs[:, u, i, j : j + 1]
+                if vector:
                     nc.vector.tensor_scalar(out=xw[u][:, i, cols], in0=src, scalar1=sc, scalar2=None, op0=ALU.mult)
                 else:
                     nc.scalar.activation(out=xw[u][:, i, cols], in_=src, func=ACT.Copy, scale=sc)
 
         def turn(u, i):
-            xt[u, i] = psum.tile([P, 2, 2, P], F32, name="xt", bufs=2)
+            xt[u, i] = psum.tile([P, 2, 2, P], F32, name="xt", bufs=XTB)
             words = xw[u][:, i, :].bitcast(F32)
             for g in range(2):
                 for e in range(2):
@@ -110,123 +131,136 @@ def tile_charformersoftsubwordblockmixer_d1p_kernel(
 
         def xcopy(u, i):
             if i == 0:
-                xg[u] = work.tile([P, TPU, 2, P, 2], F32, name="xg", align_bytes=64)
+                xg[u] = work.tile([P, TPU, 2, P, 2], F32, name="xg", bufs=4, align_bytes=64)
             nc.scalar.copy(out=xg[u][:, i], in_=xt[u, i][:].rearrange("p g e r -> p g r e"))
 
         def quant_x(u, i):
             if i == 0:
-                xc[u] = work.tile([P, TPU, 2, P], U32, name="xc", align_bytes=64)
-                xsc[u] = work.tile([P, TPU, 2, P], U8, name="xsc", align_bytes=64)
+                xc[u] = work.tile([P, TPU, 2, P], U32, name="xc", bufs=5, align_bytes=64)
+                xsc[u] = work.tile([P, TPU, 2, P], U8, name="xsc", bufs=5, align_bytes=64)
             nc.vector.quantize_mx(
                 out=xc[u][:, i].rearrange("p g r -> p (g r)").bitcast(F8X4),
                 scales=xsc[u][:, i].rearrange("p g r -> p (g r)"),
                 in_=xg[u][:, i].rearrange("p g r e -> p (g r e)").bitcast(BF16),
             )
 
-        def stage1(u, i):
-            for n in range(2):
-                hp[u, i, n] = psum.tile([P, 512], F32, name="mm", bufs=3)
-                cols = slice(512 * n, 512 * n + 512)
-                for g in range(2):
-                    nc.tensor.matmul_mx(
-                        out=hp[u, i, n][:],
-                        lhsT=xc[u][:, i, g, :].bitcast(F8X4),
-                        lhsT_scale=xsc[u][:, i, g, :],
-                        rhs=w1c[:, g, cols].bitcast(F8X4),
-                        rhs_scale=w1s[4 * g : P, cols],
-                        start=(g == 0),
-                        stop=(g == 1),
-                    )
-                if n == 0:
-                    hcopy(u, i, 0)
-            hcopy(u, i, 1)
+        def stage1(u, i, n):
+            hp[u, i, n] = psum.tile([P, 512], F32, name="mm", bufs=MMB)
+            cols = slice(512 * n, 512 * n + 512)
+            for g in range(2):
+                nc.tensor.matmul_mx(
+                    out=hp[u, i, n][:],
+                    lhsT=xc[u][:, i, g, :].bitcast(F8X4),
+                    lhsT_scale=xsc[u][:, i, g, :],
+                    rhs=w1c[:, g, cols].bitcast(F8X4),
+                    rhs_scale=w1s[4 * g : P, cols],
+                    start=(g == 0),
+                    stop=(g == 1),
+                )
 
         def hcopy(u, i, n):
-            if i == 0 and n == 0:
-                hsb[u] = work.tile([P, TPU, F], F32, name="hsb", bufs=4, align_bytes=64)
-            nc.scalar.copy(
-                out=hsb[u][:, i, 512 * n : 512 * n + 512].rearrange("q (t p) -> q t p", t=4),
-                in_=hp[u, i, n][:].rearrange("q (p t) -> q t p", t=4),
-            )
+            cols = slice(512 * n, 512 * n + 512)
+            if i == 0:
+                if n == 0:
+                    he[u] = work.tile([P, F], F32, name="he", bufs=5, align_bytes=64)
+                nc.scalar.copy(out=he[u][:, cols], in_=hp[u, i, n][:])
+            else:
+                if n == 0:
+                    hs[u] = work.tile([P, F], F32, name="hs", bufs=5, align_bytes=64)
+                nc.vector.tensor_tensor(out=hs[u][:, cols], in0=hp[u, i, n][:], in1=he[u][:, cols], op=ALU.add)
 
         def score(u, i):
-            if i == 0:
-                sv[u] = small.tile([P, TPU], F32, name="sv")
+            s_t[u, i] = small.tile([P, 1], F32, name="s%d" % i)
             junk = work.tile([P, F], F32, name="junk", bufs=2)
             nc.vector.scalar_tensor_tensor(
-                out=junk[:], in0=hsb[u][:, i, :], scalar=1.0, in1=wsb[:],
-                op0=ALU.mult, op1=ALU.mult, accum_out=sv[u][:, i : i + 1],
+                out=junk[:], in0=(he, hs)[i][u][:], scalar=1.0, in1=wsb[:],
+                op0=ALU.mult, op1=ALU.mult, accum_out=s_t[u, i][:],
             )
 
-        def spread(u):
-            rs[u] = small.tile([P, TPU, 32], F32, name="rs", align_bytes=64)
-            nc.vector.tensor_tensor(
-                out=rs[u][:],
-                in0=rm[:].rearrange("p r b -> p (r b)").unsqueeze(1).to_broadcast([P, TPU, 32]),
-                in1=sv[u][:].unsqueeze(2).to_broadcast([P, TPU, 32]),
-                op=ALU.mult,
-            )
+        def spread(u, i):
+            if i == 0:
+                r0[u] = small.tile([P, 32], F32, name="r0")
+                nc.vector.tensor_scalar(
+                    out=r0[u][:], in0=md[:].rearrange("p r b -> p (r b)"), scalar1=s_t[u, 0][:], scalar2=None, op0=ALU.mult
+                )
+            else:
+                rs[u] = small.tile([P, 32], F32, name="rs", align_bytes=64)
+                nc.vector.scalar_tensor_tensor(
+                    out=rs[u][:], in0=mo[:].rearrange("p r b -> p (r b)"), scalar=s_t[u, 1][:], in1=r0[u][:],
+                    op0=ALU.mult, op1=ALU.add,
+                )
 
         def gather(u):
-            sc[u] = psum.tile([P, 64], F32, name="sc", bufs=1)
+            sc[u] = psum.tile([P, 8, 4], F32, name="sc", bufs=1)
             nc.tensor.matmul(
-                sc[u][:], lhsT=bones[:].rearrange("p g r -> p (g r)"),
-                rhs=rs[u][:].rearrange("p i c -> p (i c)"), start=True, stop=True,
+                sc[u][:].rearrange("p r b -> p (r b)"), lhsT=bones[:].rearrange("p g r -> p (g r)"),
+                rhs=rs[u][:], start=True, stop=True,
             )
 
-        def soft_a(u):
-            s3 = sc[u][:].rearrange("p (m b) -> p m b", b=4)
-            mx = small.tile([P, 16], F32, name="mx")
-            nc.vector.tensor_reduce(out=mx[:], in_=s3, axis=AX.X, op=ALU.max)
-            df = small.tile([P, 16, 4], F32, name="df")
-            nc.vector.tensor_tensor(out=df[:], in0=s3, in1=mx[:].unsqueeze(2).to_broadcast([P, 16, 4]), op=ALU.subtract)
-            ek[u] = small.tile([P, 2, 64], F32, name="ek")
-            nc.scalar.activation(out=ek[u][:, 0, :], in_=df[:].rearrange("p m b -> p (m b)"), func=ACT.Exp)
-
-        def soft_b(u):
-            nc.vector.tensor_tensor(
-                out=ek[u][:, 1, :].rearrange("p (i c) -> p i c", i=TPU),
-                in0=ek[u][:, 0, :].rearrange("p (i c) -> p i c", i=TPU),
-                in1=rm[:].rearrange("p r b -> p (r b)").unsqueeze(1).to_broadcast([P, TPU, 32]),
-                op=ALU.mult,
-            )
-            dn = small.tile([P, 32], F32, name="dn")
-            nc.vector.tensor_reduce(out=dn[:], in_=ek[u][:].rearrange("p c (m b) -> p (c m) b", b=4), axis=AX.X, op=ALU.add)
-            rd = small.tile([P, 16], F32, name="rd")
-            nc.vector.reciprocal(out=rd[:], in_=dn[:, 0:16])
-            wt = small.tile([P, 16], F32, name="wt")
-            nc.vector.tensor_tensor(out=wt[:], in0=dn[:, 16:32], in1=rd[:], op=ALU.mult)
-            cc = small.tile([P, TPU, 4], F32, name="cc")
-            nc.vector.tensor_reduce(
-                out=cc[:].rearrange("p i j -> p (i j)"), in_=wt[:].rearrange("p (m r) -> p m r", r=2), axis=AX.X, op=ALU.add
-            )
-            ct[u] = small.tile([P, TPU, 16, 4], F32, name="ct", align_bytes=64)
-            nc.vector.tensor_tensor(
-                out=ct[u][:],
-                in0=gm[:].unsqueeze(1).unsqueeze(3).to_broadcast([P, TPU, 16, 4]),
-                in1=cc[:].unsqueeze(2).to_broadcast([P, TPU, 16, 4]),
-                op=ALU.mult,
-            )
+        def soft(u, n):
+            if n == 0:
+                mx[u] = small.tile([P, 8], F32, name="mx")
+                nc.vector.tensor_reduce(out=mx[u][:], in_=sc[u][:], axis=AX.X, op=ALU.max)
+            elif n == 1:
+                df[u] = small.tile([P, 8, 4], F32, name="df")
+                nc.vector.tensor_tensor(out=df[u][:], in0=sc[u][:], in1=mx[u][:].unsqueeze(2).to_broadcast([P, 8, 4]), op=ALU.subtract)
+            elif n == 2:
+                ex[u] = small.tile([P, 8, 4], F32, name="ex")
+                nc.scalar.activation(out=ex[u][:], in_=df[u][:], func=ACT.Exp)
+            elif n == 3:
+                dn[u] = small.tile([P, 8], F32, name="dn")
+                nc.vector.tensor_reduce(out=dn[u][:], in_=ex[u][:], axis=AX.X, op=ALU.add)
+            elif n == 4:
+                rd[u] = small.tile([P, 8], F32, name="rd")
+                nc.vector.reciprocal(out=rd[u][:], in_=dn[u][:])
+            elif n == 5:
+                aw[u] = small.tile([P, 8, 4], F32, name="aw")
+                nc.vector.tensor_tensor(out=aw[u][:], in0=ex[u][:], in1=rd[u][:].unsqueeze(2).to_broadcast([P, 8, 4]), op=ALU.mult)
+            elif n == 6:
+                ak[u] = small.tile([P, 8, 4], F32, name="ak")
+                nc.vector.tensor_tensor(out=ak[u][:], in0=aw[u][:], in1=mo[:], op=ALU.mult)
+            elif n == 7:
+                cc[u] = small.tile([P, 4], F32, name="cc")
+                nc.vector.tensor_reduce(out=cc[u][:], in_=ak[u][:].rearrange("p (j r) b -> p j (r b)", r=2), axis=AX.X, op=ALU.add)
+            elif n == 8:
+                ct[u] = small.tile([P, 32, 4], F32, name="ct", align_bytes=64)
+                nc.vector.tensor_tensor(
+                    out=ct[u][:], in0=gm[:].unsqueeze(2).to_broadcast([P, 32, 4]),
+                    in1=cc[u][:].unsqueeze(1).to_broadcast([P, 32, 4]), op=ALU.mult,
+                )
+            elif n == 9:
+                de[u] = small.tile([P, 1], F32, name="de")
+                j8 = small.tile([P, 8], F32, name="j8")
+                nc.vector.scalar_tensor_tensor(
+                    out=j8[:], in0=aw[u][:, :, 0], scalar=0.5, in1=md[:, :, 0], op0=ALU.mult, op1=ALU.mult, accum_out=de[u][:]
+                )
 
         def mix(u, g):
-            mp[u, g] = psum.tile([P, 4, TPU, 64], F32, name="mp", bufs=2)
-            for i in range(TPU):
-                for t in range(4):
-                    c0 = 512 * g + 128 * t
-                    nc.tensor.matmul(
-                        mp[u, g][:, t, i, :], lhsT=hsb[u][:, i, c0 : c0 + 128],
-                        rhs=ct[u][:, i].rearrange("p a b -> p (a b)"), start=True, stop=True,
-                    )
-
-        def add_bias(u, g):
-            if g == 0:
-                dg[u] = work.tile([P, 2, P, 4], BF16, name="dg", align_bytes=64)
-            nc.vector.tensor_tensor(
-                out=dg[u][:, g],
-                in0=mp[u, g][:].rearrange("p t i n -> p (i n) t"),
-                in1=b1pt[:, g, :].unsqueeze(1).to_broadcast([P, P, 4]),
-                op=ALU.add,
+            mp[u, g] = psum.tile([P, 512], F32, name="mp", bufs=MPB)
+            cols = slice(512 * g, 512 * g + 512)
+            nc.tensor.matmul(mp[u, g][:], lhsT=ones[:], rhs=brow[:, cols], start=True, stop=False)
+            nc.tensor.matmul(
+                mp[u, g][:], lhsT=ct[u][:].rearrange("p a b -> p (a b)"), rhs=hs[u][:, cols], start=False, stop=True
             )
+
+        def pair_mean(u, g):
+            if g == 0:
+                db[u] = work.tile([P, F], BF16, name="db", bufs=4, align_bytes=64)
+            cols = slice(512 * g, 512 * g + 512)
+            nc.vector.scalar_tensor_tensor(
+                out=db[u][:, cols], in0=he[u][:, cols], scalar=de[u][:], in1=mp[u, g][:], op0=ALU.mult, op1=ALU.add
+            )
+
+        def turn_d(u):
+            dt[u] = psum.tile([P, 2, 2, P], F32, name="xt", bufs=XTB)
+            words = db[u][:].bitcast(F32)
+            for g in range(2):
+                for e in range(2):
+                    nc.tensor.transpose(dt[u][:, g, e, :], words[:, 256 * g + e : 256 * (g + 1) : 2], ident[:])
+
+        def dcopy(u):
+            dg[u] = work.tile([P, 2, P, 2], F32, name="dg", align_bytes=64)
+            nc.scalar.copy(out=dg[u][:], in_=dt[u][:].rearrange("p g e r -> p g r e"))
 
         def quant_d(u):
             dc[u] = work.tile([P, 2, P], U32, name="dc", align_bytes=64)
@@ -234,11 +268,11 @@ def tile_charformersoftsubwordblockmixer_d1p_kernel(
             nc.vector.quantize_mx(
                 out=dc[u][:].rearrange("p g r -> p (g r)").bitcast(F8X4),
                 scales=dsc[u][:].rearrange("p g r -> p (g r)"),
-                in_=dg[u][:].rearrange("p g r e -> p (g r e)"),
+                in_=dg[u][:].rearrange("p g r e -> p (g r e)").bitcast(BF16),
             )
 
         def stage2(u, n):
-            om[u, n] = psum.tile([P, 512], F32, name="mm", bufs=3)
+            om[u, n] = psum.tile([P, 512], F32, name="mm", bufs=MMB)
             cols = slice(512 * n, 512 * n + 512)
             for g in range(2):
                 nc.tensor.matmul_mx(
@@ -258,6 +292,14 @@ def tile_charformersoftsubwordblockmixer_d1p_kernel(
             if n == 1:
                 nc.sync.dma_start(out=out_rows[u], in_=osb[u][:])
 
+        def spread_ws(n):
+            cols = slice(512 * n, 512 * n + 512)
+            wp = psum.tile([P, 512], F32, name="mm", bufs=MMB)
+            nc.tensor.matmul(wp[:], lhsT=ones[:], rhs=wrow[:, cols], start=True, stop=True)
+            nc.scalar.copy(
+                out=wsb[:, cols], in_=wp[:]
+            )
+
         def load_scales(tile, dram):
             for q in range(4):
                 nc.sync.dma_start(
@@ -272,61 +314,60 @@ def tile_charformersoftsubwordblockmixer_d1p_kernel(
                 )
 
         ops = {
-            "widen": widen, "turn": turn, "xcopy": xcopy, "quant_x": quant_x, "stage1": stage1, "score": score,
-            "spread": spread, "gather": gather, "soft_a": soft_a, "soft_b": soft_b, "mix": mix, "add_bias": add_bias,
+            "widen": widen, "turn": turn, "xcopy": xcopy, "quant_x": quant_x, "stage1": stage1, "hcopy": hcopy, "score": score,
+            "spread": spread, "gather": gather, "soft": soft, "mix": mix, "pair_mean": pair_mean, "turn_d": turn_d, "dcopy": dcopy,
             "quant_d": quant_d, "stage2": stage2, "ocopy": ocopy,
         }
 
         with tc.manual_schedule():
-            nc.scalar.dma_start(out=xs[:], in_=x_scale.flatten_outer_dims().rearrange("(n p) s -> p n s", p=P))
+            nc.scalar.dma_start(out=xs[:], in_=x_scale.flatten_outer_dims().rearrange("(u p i) s -> p u i s", i=TPU, p=P))
             load_x(0)
             make_identity(nc, ident[:])
             nc.vector.memset(w1s[:].bitcast(I32), 0)
             nc.vector.memset(w2s[:].bitcast(I32), 0)
             nc.vector.memset(wrow[:].bitcast(I32), 0)
+            nc.vector.memset(brow[:].bitcast(I32), 0)
             nc.vector.memset(ones[:], 1.0)
             nc.vector.memset(warm[:], 0.0)
             nc.scalar.dma_start(out=wrow[0:1, :], in_=ws.rearrange("(o f) -> o f", o=1))
-            nc.scalar.dma_start(out=b1pt[:], in_=b1.rearrange("(g p t) -> p g t", p=P, t=4))
+            nc.scalar.dma_start(out=brow[0:1, :], in_=b1.rearrange("(o f) -> o f", o=1))
             nc.scalar.activation(out=warm[:], in_=warm[:], func=ACT.Exp)
+            load_x(1)
             load_scales(w1s, w1_scales)
             load_scales(w2s, w2_scales)
             load_words(w1c, w1_words)
-            load_x(1)
             load_x(2)
             load_x(3)
             load_words(w2c, w2_words)
             for u in range(4, NU):
                 load_x(u)
 
-            nc.vector.tensor_reduce(out=r1[:], in_=ident[:].rearrange("p (g r) -> p r g", r=8), axis=AX.X, op=ALU.add)
-            nc.vector.tensor_reduce(out=g16[:], in_=ident[:].rearrange("p (g r) -> p g r", r=8), axis=AX.X, op=ALU.add)
-            nc.vector.tensor_reduce(out=p2[:], in_=r1[:].rearrange("p (q c) -> p q c", c=2), axis=AX.X, op=ALU.add)
-            nc.vector.tensor_reduce(out=p4[:], in_=p2[:].rearrange("p (q c) -> p q c", c=2), axis=AX.X, op=ALU.add)
-            nc.vector.tensor_copy(out=rm[:, :, 0], in_=r1[:])
+            nc.vector.tensor_reduce(out=q4[:], in_=ident[:].rearrange("p (g j) -> p j g", j=4), axis=AX.X, op=ALU.add)
+            nc.vector.tensor_reduce(out=g32[:], in_=ident[:].rearrange("p (g j) -> p g j", j=4), axis=AX.X, op=ALU.add)
+            nc.vector.memset(md[:], 0.0)
+            nc.vector.memset(mo[:, :, 0], 0.0)
+            nc.vector.memset(mo[:, :, 3], 0.125)
+            nc.vector.tensor_scalar(out=gm[:], in0=g32[:], scalar1=0.5, scalar2=None, op0=ALU.mult)
+            nc.vector.tensor_copy(out=bones[:], in_=g32[:].unsqueeze(2).to_broadcast([P, 32, 4]))
+            nc.vector.tensor_reduce(out=h2[:], in_=q4[:].rearrange("p (q c) -> p q c", c=2), axis=AX.X, op=ALU.add)
+            nc.vector.tensor_copy(out=mo[:, 1::2, 0], in_=q4[:])
+            nc.vector.tensor_copy(out=md[:, 0::2, 0], in_=q4[:])
+            nc.vector.tensor_scalar(out=md[:, 1::2, 0], in0=q4[:], scalar1=-1.0, scalar2=None, op0=ALU.mult)
             nc.vector.tensor_scalar(
-                out=rm[:, :, 1].rearrange("p (q c) -> p q c", c=2), in0=p2[:].unsqueeze(2).to_broadcast([P, 4, 2]),
+                out=mo[:, :, 1].rearrange("p (q c) -> p q c", c=2), in0=q4[:].unsqueeze(2).to_broadcast([P, 4, 2]),
                 scalar1=0.5, scalar2=None, op0=ALU.mult,
             )
             nc.vector.tensor_scalar(
-                out=rm[:, :, 2].rearrange("p (q c) -> p q c", c=4), in0=p4[:].unsqueeze(2).to_broadcast([P, 2, 4]),
+                out=mo[:, :, 2].rearrange("p (q c) -> p q c", c=4), in0=h2[:].unsqueeze(2).to_broadcast([P, 2, 4]),
                 scalar1=0.25, scalar2=None, op0=ALU.mult,
             )
-            nc.vector.memset(rm[:, :, 3], 0.125)
-            nc.vector.tensor_scalar(out=gm[:], in0=g16[:], scalar1=0.5, scalar2=None, op0=ALU.mult)
-            nc.vector.tensor_copy(out=bones[:], in_=g16[:].unsqueeze(2).to_broadcast([P, 16, 8]))
-
-            for n in range(2):
-                cols = slice(512 * n, 512 * n + 512)
-                wp = psum.tile([P, 512], F32, name="mm", bufs=3)
-                nc.tensor.matmul(wp[:], lhsT=ones[:], rhs=wrow[:, cols], start=True, stop=True)
-                nc.scalar.copy(
-                    out=wsb[:, cols].rearrange("q (t p) -> q t p", t=4), in_=wp[:].rearrange("q (p t) -> q t p", t=4)
-                )
 
             first = -max(lag for name, lag, args in STEP)
             last = NU - min(lag for name, lag, args in STEP)
             for k in range(first, last):
+                if k == WS_STEP:
+                    spread_ws(0)
+                    spread_ws(1)
                 for name, lag, args in STEP:
                     if 0 <= k + lag < NU:
                         ops[name](k + lag, *args)

from contextlib import ExitStack

import concourse.mybir as mybir
from concourse.masks import make_identity

F32 = mybir.dt.float32
BF16 = mybir.dt.bfloat16
U32 = mybir.dt.uint32
I32 = mybir.dt.int32
U8 = mybir.dt.uint8
F8 = mybir.dt.float8_e4m3fn
F8X4 = mybir.dt.float8_e4m3fn_x4
ALU = mybir.AluOpType
ACT = mybir.ActivationFunctionType
AX = mybir.AxisListType

P = 128
TOKENS, D, F, DO = 2048, 1024, 1024, 1024
NU = 8
TPU = 2
FLOPS = 2 * TOKENS * D * F + 2 * (TOKENS // 2) * F * DO
WS_STEP = 0
MMB, XTB, MPB = 3, 2, 2
VW = (5, 5, 7, 8, 3, 6, 4, 5)
STEP = (
    ("soft", -2, (3,)),
    ("turn", 0, (0,)),
    ("score", -1, (0,)),
    ("mix", -3, (1,)),
    ("turn", 0, (1,)),
    ("soft", -2, (4,)),
    ("xcopy", 0, (0,)),
    ("score", -1, (1,)),
    ("quant_x", 0, (0,)),
    ("soft", -2, (5,)),
    ("stage2", -5, (0,)),
    ("spread", -1, (0,)),
    ("xcopy", 0, (1,)),
    ("soft", -2, (6,)),
    ("spread", -1, (1,)),
    ("pair_mean", -3, (0,)),
    ("ocopy", -5, (0,)),
    ("soft", -2, (7,)),
    ("stage2", -5, (1,)),
    ("quant_x", 0, (1,)),
    ("soft", -2, (8,)),
    ("pair_mean", -3, (1,)),
    ("stage1", 0, (0, 0)),
    ("ocopy", -5, (1,)),
    ("widen", 1, (0, True)),
    ("hcopy", 0, (0, 0)),
    ("gather", -1, ()),
    ("stage1", 0, (0, 1)),
    ("stage1", 0, (1, 0)),
    ("widen", 1, (1, True)),
    ("soft", -1, (0,)),
    ("hcopy", 0, (0, 1)),
    ("quant_d", -4, ()),
    ("soft", -1, (1,)),
    ("soft", -1, (2,)),
    ("widen", 2, (0, False)),
    ("stage1", 0, (1, 1)),
    ("soft", -2, (9,)),
    ("mix", -2, (0,)),
    ("turn_d", -3, ()),
    ("hcopy", 0, (1, 0)),
    ("hcopy", 0, (1, 1)),
    ("widen", 2, (1, False)),
    ("dcopy", -3, ()),
)


def tile_charformersoftsubwordblockmixer_d1p_kernel(
    tc, x_bytes, x_scale, w1_words, w1_scales, b1, ws, w2_words, w2_scales, out
):
    nc = tc.nc
    with ExitStack() as ctx:
        keep = ctx.enter_context(tc.tile_pool(name="keep", bufs=1))
        xin = ctx.enter_context(tc.tile_pool(name="xin", bufs=8))
        work = ctx.enter_context(tc.tile_pool(name="work", bufs=3))
        small = ctx.enter_context(tc.tile_pool(name="small", bufs=6))
        psum = ctx.enter_context(tc.psum_pool(name="psum", bufs=1))

        x_rows = x_bytes.flatten_outer_dims().rearrange("(u p i) d -> u p i d", i=TPU, p=P)
        out_rows = out.flatten_outer_dims().rearrange("(u p) d -> u p d", p=P)

        ident = keep.tile([P, P], F32, name="ident", align_bytes=64)
        xs = keep.tile([P, NU, TPU, 8], F32, name="xs")
        w1c = keep.tile([P, 2, F], U32, name="w1c", align_bytes=64)
        w2c = keep.tile([P, 2, DO], U32, name="w2c", align_bytes=64)
        w1s = keep.tile([P, F], U8, name="w1s", align_bytes=64)
        w2s = keep.tile([P, DO], U8, name="w2s", align_bytes=64)
        wrow = keep.tile([P, F], BF16, name="wrow", align_bytes=64)
        ones = keep.tile([P, P], BF16, name="ones", align_bytes=64)
        wsb = keep.tile([P, F], F32, name="wsb", align_bytes=64)
        brow = keep.tile([P, F], BF16, name="brow", align_bytes=64)
        q4 = keep.tile([P, 4], F32, name="q4")
        h2 = keep.tile([P, 2], F32, name="h2")
        mo = keep.tile([P, 8, 4], F32, name="mo")
        md = keep.tile([P, 8, 4], F32, name="md")
        g32 = keep.tile([P, 32], F32, name="g32")
        gm = keep.tile([P, 32], F32, name="gm")
        bones = keep.tile([P, 32, 4], F32, name="bones", align_bytes=64)
        warm = keep.tile([P, 1], F32, name="warm")

        xb, xw, xt, xg, xc, xsc, hp, he, hs, s_t, r0, rs, sc = ({} for _ in range(13))
        mx, df, ex, dn, rd, aw, ak, cc, ct, de, mp, db, dt, dg, dc, dsc, om, osb = ({} for _ in range(18))

        def load_x(u):
            xb[u] = xin.tile([P, TPU, D], U8, name="xb", align_bytes=64)
            nc.sync.dma_start(out=xb[u][:], in_=x_rows[u])

        def widen(u, i, vector):
            if u not in xw:
                xw[u] = work.tile([P, TPU, D], BF16, name="xw", bufs=4, align_bytes=64)
            for j in range(0, VW[u]) if vector else range(VW[u], 8):
                cols = slice(128 * j, 128 * j + 128)
                src = xb[u][:, i, cols].bitcast(F8)
                sc = xs[:, u, i, j : j + 1]
                if vector:
                    nc.vector.tensor_scalar(out=xw[u][:, i, cols], in0=src, scalar1=sc, scalar2=None, op0=ALU.mult)
                else:
                    nc.scalar.activation(out=xw[u][:, i, cols], in_=src, func=ACT.Copy, scale=sc)

        def turn(u, i):
            xt[u, i] = psum.tile([P, 2, 2, P], F32, name="xt", bufs=XTB)
            words = xw[u][:, i, :].bitcast(F32)
            for g in range(2):
                for e in range(2):
                    nc.tensor.transpose(xt[u, i][:, g, e, :], words[:, 256 * g + e : 256 * (g + 1) : 2], ident[:])

        def xcopy(u, i):
            if i == 0:
                xg[u] = work.tile([P, TPU, 2, P, 2], F32, name="xg", bufs=4, align_bytes=64)
            nc.scalar.copy(out=xg[u][:, i], in_=xt[u, i][:].rearrange("p g e r -> p g r e"))

        def quant_x(u, i):
            if i == 0:
                xc[u] = work.tile([P, TPU, 2, P], U32, name="xc", bufs=5, align_bytes=64)
                xsc[u] = work.tile([P, TPU, 2, P], U8, name="xsc", bufs=5, align_bytes=64)
            nc.vector.quantize_mx(
                out=xc[u][:, i].rearrange("p g r -> p (g r)").bitcast(F8X4),
                scales=xsc[u][:, i].rearrange("p g r -> p (g r)"),
                in_=xg[u][:, i].rearrange("p g r e -> p (g r e)").bitcast(BF16),
            )

        def stage1(u, i, n):
            hp[u, i, n] = psum.tile([P, 512], F32, name="mm", bufs=MMB)
            cols = slice(512 * n, 512 * n + 512)
            for g in range(2):
                nc.tensor.matmul_mx(
                    out=hp[u, i, n][:],
                    lhsT=xc[u][:, i, g, :].bitcast(F8X4),
                    lhsT_scale=xsc[u][:, i, g, :],
                    rhs=w1c[:, g, cols].bitcast(F8X4),
                    rhs_scale=w1s[4 * g : P, cols],
                    start=(g == 0),
                    stop=(g == 1),
                )

        def hcopy(u, i, n):
            cols = slice(512 * n, 512 * n + 512)
            if i == 0:
                if n == 0:
                    he[u] = work.tile([P, F], F32, name="he", bufs=5, align_bytes=64)
                nc.scalar.copy(out=he[u][:, cols], in_=hp[u, i, n][:])
            else:
                if n == 0:
                    hs[u] = work.tile([P, F], F32, name="hs", bufs=5, align_bytes=64)
                nc.vector.tensor_tensor(out=hs[u][:, cols], in0=hp[u, i, n][:], in1=he[u][:, cols], op=ALU.add)

        def score(u, i):
            s_t[u, i] = small.tile([P, 1], F32, name="s%d" % i)
            junk = work.tile([P, F], F32, name="junk", bufs=2)
            nc.vector.scalar_tensor_tensor(
                out=junk[:], in0=(he, hs)[i][u][:], scalar=1.0, in1=wsb[:],
                op0=ALU.mult, op1=ALU.mult, accum_out=s_t[u, i][:],
            )

        def spread(u, i):
            if i == 0:
                r0[u] = small.tile([P, 32], F32, name="r0")
                nc.vector.tensor_scalar(
                    out=r0[u][:], in0=md[:].rearrange("p r b -> p (r b)"), scalar1=s_t[u, 0][:], scalar2=None, op0=ALU.mult
                )
            else:
                rs[u] = small.tile([P, 32], F32, name="rs", align_bytes=64)
                nc.vector.scalar_tensor_tensor(
                    out=rs[u][:], in0=mo[:].rearrange("p r b -> p (r b)"), scalar=s_t[u, 1][:], in1=r0[u][:],
                    op0=ALU.mult, op1=ALU.add,
                )

        def gather(u):
            sc[u] = psum.tile([P, 8, 4], F32, name="sc", bufs=1)
            nc.tensor.matmul(
                sc[u][:].rearrange("p r b -> p (r b)"), lhsT=bones[:].rearrange("p g r -> p (g r)"),
                rhs=rs[u][:], start=True, stop=True,
            )

        def soft(u, n):
            if n == 0:
                mx[u] = small.tile([P, 8], F32, name="mx")
                nc.vector.tensor_reduce(out=mx[u][:], in_=sc[u][:], axis=AX.X, op=ALU.max)
            elif n == 1:
                df[u] = small.tile([P, 8, 4], F32, name="df")
                nc.vector.tensor_tensor(out=df[u][:], in0=sc[u][:], in1=mx[u][:].unsqueeze(2).to_broadcast([P, 8, 4]), op=ALU.subtract)
            elif n == 2:
                ex[u] = small.tile([P, 8, 4], F32, name="ex")
                nc.scalar.activation(out=ex[u][:], in_=df[u][:], func=ACT.Exp)
            elif n == 3:
                dn[u] = small.tile([P, 8], F32, name="dn")
                nc.vector.tensor_reduce(out=dn[u][:], in_=ex[u][:], axis=AX.X, op=ALU.add)
            elif n == 4:
                rd[u] = small.tile([P, 8], F32, name="rd")
                nc.vector.reciprocal(out=rd[u][:], in_=dn[u][:])
            elif n == 5:
                aw[u] = small.tile([P, 8, 4], F32, name="aw")
                nc.vector.tensor_tensor(out=aw[u][:], in0=ex[u][:], in1=rd[u][:].unsqueeze(2).to_broadcast([P, 8, 4]), op=ALU.mult)
            elif n == 6:
                ak[u] = small.tile([P, 8, 4], F32, name="ak")
                nc.vector.tensor_tensor(out=ak[u][:], in0=aw[u][:], in1=mo[:], op=ALU.mult)
            elif n == 7:
                cc[u] = small.tile([P, 4], F32, name="cc")
                nc.vector.tensor_reduce(out=cc[u][:], in_=ak[u][:].rearrange("p (j r) b -> p j (r b)", r=2), axis=AX.X, op=ALU.add)
            elif n == 8:
                ct[u] = small.tile([P, 32, 4], F32, name="ct", align_bytes=64)
                nc.vector.tensor_tensor(
                    out=ct[u][:], in0=gm[:].unsqueeze(2).to_broadcast([P, 32, 4]),
                    in1=cc[u][:].unsqueeze(1).to_broadcast([P, 32, 4]), op=ALU.mult,
                )
            elif n == 9:
                de[u] = small.tile([P, 1], F32, name="de")
                j8 = small.tile([P, 8], F32, name="j8")
                nc.vector.scalar_tensor_tensor(
                    out=j8[:], in0=aw[u][:, :, 0], scalar=0.5, in1=md[:, :, 0], op0=ALU.mult, op1=ALU.mult, accum_out=de[u][:]
                )

        def mix(u, g):
            mp[u, g] = psum.tile([P, 512], F32, name="mp", bufs=MPB)
            cols = slice(512 * g, 512 * g + 512)
            nc.tensor.matmul(mp[u, g][:], lhsT=ones[:], rhs=brow[:, cols], start=True, stop=False)
            nc.tensor.matmul(
                mp[u, g][:], lhsT=ct[u][:].rearrange("p a b -> p (a b)"), rhs=hs[u][:, cols], start=False, stop=True
            )

        def pair_mean(u, g):
            if g == 0:
                db[u] = work.tile([P, F], BF16, name="db", bufs=4, align_bytes=64)
            cols = slice(512 * g, 512 * g + 512)
            nc.vector.scalar_tensor_tensor(
                out=db[u][:, cols], in0=he[u][:, cols], scalar=de[u][:], in1=mp[u, g][:], op0=ALU.mult, op1=ALU.add
            )

        def turn_d(u):
            dt[u] = psum.tile([P, 2, 2, P], F32, name="xt", bufs=XTB)
            words = db[u][:].bitcast(F32)
            for g in range(2):
                for e in range(2):
                    nc.tensor.transpose(dt[u][:, g, e, :], words[:, 256 * g + e : 256 * (g + 1) : 2], ident[:])

        def dcopy(u):
            dg[u] = work.tile([P, 2, P, 2], F32, name="dg", align_bytes=64)
            nc.scalar.copy(out=dg[u][:], in_=dt[u][:].rearrange("p g e r -> p g r e"))

        def quant_d(u):
            dc[u] = work.tile([P, 2, P], U32, name="dc", align_bytes=64)
            dsc[u] = work.tile([P, 2, P], U8, name="dsc", align_bytes=64)
            nc.vector.quantize_mx(
                out=dc[u][:].rearrange("p g r -> p (g r)").bitcast(F8X4),
                scales=dsc[u][:].rearrange("p g r -> p (g r)"),
                in_=dg[u][:].rearrange("p g r e -> p (g r e)").bitcast(BF16),
            )

        def stage2(u, n):
            om[u, n] = psum.tile([P, 512], F32, name="mm", bufs=MMB)
            cols = slice(512 * n, 512 * n + 512)
            for g in range(2):
                nc.tensor.matmul_mx(
                    out=om[u, n][:],
                    lhsT=dc[u][:, g, :].bitcast(F8X4),
                    lhsT_scale=dsc[u][:, g, :],
                    rhs=w2c[:, g, cols].bitcast(F8X4),
                    rhs_scale=w2s[4 * g : P, cols],
                    start=(g == 0),
                    stop=(g == 1),
                )

        def ocopy(u, n):
            if n == 0:
                osb[u] = work.tile([P, DO], F32, name="osb", align_bytes=64)
            nc.scalar.copy(out=osb[u][:, 512 * n : 512 * n + 512], in_=om[u, n][:])
            if n == 1:
                nc.sync.dma_start(out=out_rows[u], in_=osb[u][:])

        def spread_ws(n):
            cols = slice(512 * n, 512 * n + 512)
            wp = psum.tile([P, 512], F32, name="mm", bufs=MMB)
            nc.tensor.matmul(wp[:], lhsT=ones[:], rhs=wrow[:, cols], start=True, stop=True)
            nc.scalar.copy(
                out=wsb[:, cols], in_=wp[:]
            )

        def load_scales(tile, dram):
            for q in range(4):
                nc.sync.dma_start(
                    out=tile[32 * q : 32 * q + 8, :].bitcast(I32),
                    in_=dram[:, 4 * q : 4 * q + 4, :].bitcast(I32),
                )

        def load_words(tile, dram):
            for g in range(2):
                nc.sync.dma_start(
                    out=tile[:, g, :].bitcast(I32), in_=dram[g].rearrange("p n t -> p (n t)").bitcast(I32)
                )

        ops = {
            "widen": widen, "turn": turn, "xcopy": xcopy, "quant_x": quant_x, "stage1": stage1, "hcopy": hcopy, "score": score,
            "spread": spread, "gather": gather, "soft": soft, "mix": mix, "pair_mean": pair_mean, "turn_d": turn_d, "dcopy": dcopy,
            "quant_d": quant_d, "stage2": stage2, "ocopy": ocopy,
        }

        with tc.manual_schedule():
            nc.scalar.dma_start(out=xs[:], in_=x_scale.flatten_outer_dims().rearrange("(u p i) s -> p u i s", i=TPU, p=P))
            load_x(0)
            make_identity(nc, ident[:])
            nc.vector.memset(w1s[:].bitcast(I32), 0)
            nc.vector.memset(w2s[:].bitcast(I32), 0)
            nc.vector.memset(wrow[:].bitcast(I32), 0)
            nc.vector.memset(brow[:].bitcast(I32), 0)
            nc.vector.memset(ones[:], 1.0)
            nc.vector.memset(warm[:], 0.0)
            nc.scalar.dma_start(out=wrow[0:1, :], in_=ws.rearrange("(o f) -> o f", o=1))
            nc.scalar.dma_start(out=brow[0:1, :], in_=b1.rearrange("(o f) -> o f", o=1))
            nc.scalar.activation(out=warm[:], in_=warm[:], func=ACT.Exp)
            load_x(1)
            load_scales(w1s, w1_scales)
            load_scales(w2s, w2_scales)
            load_words(w1c, w1_words)
            load_x(2)
            load_x(3)
            load_words(w2c, w2_words)
            for u in range(4, NU):
                load_x(u)

            nc.vector.tensor_reduce(out=q4[:], in_=ident[:].rearrange("p (g j) -> p j g", j=4), axis=AX.X, op=ALU.add)
            nc.vector.tensor_reduce(out=g32[:], in_=ident[:].rearrange("p (g j) -> p g j", j=4), axis=AX.X, op=ALU.add)
            nc.vector.memset(md[:], 0.0)
            nc.vector.memset(mo[:, :, 0], 0.0)
            nc.vector.memset(mo[:, :, 3], 0.125)
            nc.vector.tensor_scalar(out=gm[:], in0=g32[:], scalar1=0.5, scalar2=None, op0=ALU.mult)
            nc.vector.tensor_copy(out=bones[:], in_=g32[:].unsqueeze(2).to_broadcast([P, 32, 4]))
            nc.vector.tensor_reduce(out=h2[:], in_=q4[:].rearrange("p (q c) -> p q c", c=2), axis=AX.X, op=ALU.add)
            nc.vector.tensor_copy(out=mo[:, 1::2, 0], in_=q4[:])
            nc.vector.tensor_copy(out=md[:, 0::2, 0], in_=q4[:])
            nc.vector.tensor_scalar(out=md[:, 1::2, 0], in0=q4[:], scalar1=-1.0, scalar2=None, op0=ALU.mult)
            nc.vector.tensor_scalar(
                out=mo[:, :, 1].rearrange("p (q c) -> p q c", c=2), in0=q4[:].unsqueeze(2).to_broadcast([P, 4, 2]),
                scalar1=0.5, scalar2=None, op0=ALU.mult,
            )
            nc.vector.tensor_scalar(
                out=mo[:, :, 2].rearrange("p (q c) -> p q c", c=4), in0=h2[:].unsqueeze(2).to_broadcast([P, 2, 4]),
                scalar1=0.25, scalar2=None, op0=ALU.mult,
            )

            first = -max(lag for name, lag, args in STEP)
            last = NU - min(lag for name, lag, args in STEP)
            for k in range(first, last):
                if k == WS_STEP:
                    spread_ws(0)
                    spread_ws(1)
                for name, lag, args in STEP:
                    if 0 <= k + lag < NU:
                        ops[name](k + lag, *args)
